import numpy as np
import ml_dtypes

BF16 = ml_dtypes.bfloat16


def bf(x):
    return np.asarray(x, np.float32).astype(BF16)


def f32(x):
    return np.asarray(x, np.float32)


def f64(x):
    return np.asarray(x).astype(np.float64)


def striped(idx):
    return np.tile(idx.reshape(-1, 16).T, (8, 1))


S, K, M, N, D, V = 4096, 256, 256, 2048, 2, 1024


def setup_inputs():
    return {"table": bf(np.random.standard_normal((K, S))), "w": bf(np.random.standard_normal((D, K, M)) / np.sqrt(D * K)), "b": f32(0.5 * np.random.standard_normal((M, 1))), "offs": striped(np.random.permutation(S)[:N])}


def reference(table, w, b, offs):
    idx = offs[:16].T.reshape(-1)
    x = f64(table)[:, idx]
    y = sum(f64(w)[t].T @ x[:, t * V : (t + 1) * V] for t in range(D))
    return np.tanh(y + f64(b))

@@ -1,0 +1,86 @@
+import concourse.mybir as mybir
+
+BF16, F32, U16 = mybir.dt.bfloat16, mybir.dt.float32, mybir.dt.uint16
+TANH = mybir.ActivationFunctionType.Tanh
+
+P = 128
+K, S = 256, 4096
+ENDS, M = 2, 256
+V = 1024
+PIECE = 512
+K_BLOCKS, M_BLOCKS, V_BLOCKS = K // P, M // P, V // PIECE
+HALF = PIECE // 2
+
+FLOPS = 2 * K * M * ENDS * V
+
+
+def tile_gather_matmul_kernel(tc, table, w, b, offs, out):
+    nc = tc.nc
+    with (
+        tc.tile_pool(name="held", bufs=1) as held,
+        tc.psum_pool(name="psum", bufs=1) as psum,
+    ):
+        offsets = held.tile([P, ENDS * V // 16], U16)
+        nc.sync.dma_start(offsets[:], offs)
+
+        table_blocks = [held.tile([P, S], BF16, name=f"table{kb}") for kb in range(K_BLOCKS)]
+        weights = {
+            (t, kb): held.tile([P, M], BF16, name=f"weights{t}{kb}")
+            for t in range(ENDS)
+            for kb in range(K_BLOCKS)
+        }
+        bias = held.tile([P, M_BLOCKS], F32)
+
+        w_rows = w.rearrange("t k m -> (t k) m")
+
+        def load_weights(queue, t, kb):
+            first_row = t * K + kb * P
+            queue.dma_start(weights[t, kb][:], w_rows[first_row : first_row + P, :])
+
+        load_weights(nc.scalar, 0, 0)
+        nc.scalar.dma_start(bias[:], b.rearrange("(mb p) o -> p (mb o)", p=P))
+        nc.sync.dma_start(table_blocks[0][:], table[0:P, :])
+        load_weights(nc.sync, 1, 0)
+        load_weights(nc.sync, 0, 1)
+        load_weights(nc.sync, 1, 1)
+        nc.sync.dma_start(table_blocks[1][:], table[P : 2 * P, :])
+
+        output_tiles = [(mb, vb) for mb in range(M_BLOCKS) for vb in range(V_BLOCKS)]
+        banks = {
+            (mb, vb): psum.tile([P, PIECE], F32, name=f"bank{mb}{vb}") for mb, vb in output_tiles
+        }
+        results = {
+            (mb, vb): held.tile([P, PIECE], F32, name=f"result{mb}{vb}") for mb, vb in output_tiles
+        }
+
+        def product(kb, t, mb, vb):
+            first_column = (t * V + vb * PIECE) // 16
+            piece = offsets[:, first_column : first_column + PIECE // 16]
+            nc.tensor.matmul(
+                banks[mb, vb][:],
+                weights[t, kb][:, mb * P : (mb + 1) * P],
+                table_blocks[kb][:].indirect(piece),
+                start=(kb == 0 and t == 0),
+                stop=(kb == K_BLOCKS - 1 and t == ENDS - 1),
+            )
+
+        def finish(mb, vb):
+            for first in (0, HALF):
+                nc.scalar.activation(
+                    results[mb, vb][:, first : first + HALF],
+                    banks[mb, vb][:, first : first + HALF],
+                    TANH,
+                    bias=bias[:, mb : mb + 1],
+                )
+                nc.sync.dma_start(
+                    out[mb * P : (mb + 1) * P, vb * PIECE + first : vb * PIECE + first + HALF],
+                    results[mb, vb][:, first : first + HALF],
+                )
+
+        for t in range(ENDS):
+            for mb, vb in output_tiles:
+                product(0, t, mb, vb)
+        for mb, vb in output_tiles:
+            for t in range(ENDS):
+                product(1, t, mb, vb)
+            finish(mb, vb)

@@ -24,25 +24,17 @@ def tile_gather_matmul_kernel(tc, table, w, b, offs, out):
         nc.sync.dma_start(offsets[:], offs)
 
         table_blocks = [held.tile([P, S], BF16, name=f"table{kb}") for kb in range(K_BLOCKS)]
-        weights = {
-            (t, kb): held.tile([P, M], BF16, name=f"weights{t}{kb}")
-            for t in range(ENDS)
-            for kb in range(K_BLOCKS)
-        }
+        weights = [held.tile([P, ENDS, M], BF16, name=f"weights{kb}") for kb in range(K_BLOCKS)]
         bias = held.tile([P, M_BLOCKS], F32)
 
-        w_rows = w.rearrange("t k m -> (t k) m")
+        w_by_row = w.rearrange("t k m -> k t m")
 
-        def load_weights(queue, t, kb):
-            first_row = t * K + kb * P
-            queue.dma_start(weights[t, kb][:], w_rows[first_row : first_row + P, :])
-
-        load_weights(nc.scalar, 0, 0)
+        nc.scalar.dma_start(weights[0][:, 0, 0:P], w_by_row[0:P, 0, 0:P])
         nc.scalar.dma_start(bias[:], b.rearrange("(mb p) o -> p (mb o)", p=P))
         nc.sync.dma_start(table_blocks[0][:], table[0:P, :])
-        load_weights(nc.sync, 1, 0)
-        load_weights(nc.sync, 0, 1)
-        load_weights(nc.sync, 1, 1)
+        nc.sync.dma_start(weights[0][:, 0, P:M], w_by_row[0:P, 0, P:M])
+        nc.sync.dma_start(weights[0][:, 1, :], w_by_row[0:P, 1, :])
+        nc.sync.dma_start(weights[1][:], w_by_row[P : 2 * P, :, :])
         nc.sync.dma_start(table_blocks[1][:], table[P : 2 * P, :])
 
         output_tiles = [(mb, vb) for mb in range(M_BLOCKS) for vb in range(V_BLOCKS)]
@@ -58,7 +50,7 @@ def tile_gather_matmul_kernel(tc, table, w, b, offs, out):
             piece = offsets[:, first_column : first_column + PIECE // 16]
             nc.tensor.matmul(
                 banks[mb, vb][:],
-                weights[t, kb][:, mb * P : (mb + 1) * P],
+                weights[kb][:, t, mb * P : (mb + 1) * P],
                 table_blocks[kb][:].indirect(piece),
                 start=(kb == 0 and t == 0),
                 stop=(kb == K_BLOCKS - 1 and t == ENDS - 1),

@@ -9,6 +9,7 @@ ENDS, M = 2, 256
 V = 1024
 PIECE = 512
 K_BLOCKS, M_BLOCKS, V_BLOCKS = K // P, M // P, V // PIECE
+ALIGN = 256
 HALF = PIECE // 2
 
 FLOPS = 2 * K * M * ENDS * V
@@ -20,12 +21,18 @@ def tile_gather_matmul_kernel(tc, table, w, b, offs, out):
         tc.tile_pool(name="held", bufs=1) as held,
         tc.psum_pool(name="psum", bufs=1) as psum,
     ):
-        offsets = held.tile([P, ENDS * V // 16], U16)
+        offsets = held.tile([P, ENDS * V // 16], U16, align_bytes=ALIGN)
         nc.sync.dma_start(offsets[:], offs)
 
-        table_blocks = [held.tile([P, S], BF16, name=f"table{kb}") for kb in range(K_BLOCKS)]
-        weights = [held.tile([P, ENDS, M], BF16, name=f"weights{kb}") for kb in range(K_BLOCKS)]
-        bias = held.tile([P, M_BLOCKS], F32)
+        table_blocks = [
+            held.tile([P, S], BF16, name=f"table{kb}", align_bytes=ALIGN)
+            for kb in range(K_BLOCKS)
+        ]
+        weights = [
+            held.tile([P, ENDS, M], BF16, name=f"weights{kb}", align_bytes=ALIGN)
+            for kb in range(K_BLOCKS)
+        ]
+        bias = held.tile([P, M_BLOCKS], F32, align_bytes=ALIGN)
 
         w_by_row = w.rearrange("t k m -> k t m")
 
@@ -42,7 +49,8 @@ def tile_gather_matmul_kernel(tc, table, w, b, offs, out):
             (mb, vb): psum.tile([P, PIECE], F32, name=f"bank{mb}{vb}") for mb, vb in output_tiles
         }
         results = {
-            (mb, vb): held.tile([P, PIECE], F32, name=f"result{mb}{vb}") for mb, vb in output_tiles
+            (mb, vb): held.tile([P, PIECE], F32, name=f"result{mb}{vb}", align_bytes=ALIGN)
+            for mb, vb in output_tiles
         }
 
         def product(kb, t, mb, vb):

@@ -32,12 +32,12 @@ def tile_gather_matmul_kernel(tc, table, w, b, offs, out):
             held.tile([P, ENDS, M], BF16, name=f"weights{kb}", align_bytes=ALIGN)
             for kb in range(K_BLOCKS)
         ]
-        bias = held.tile([P, M_BLOCKS], F32, align_bytes=ALIGN)
+        bias = held.tile([P, M_BLOCKS, ALIGN // 4], F32, align_bytes=ALIGN)
 
         w_by_row = w.rearrange("t k m -> k t m")
 
         nc.scalar.dma_start(weights[0][:, 0, 0:P], w_by_row[0:P, 0, 0:P])
-        nc.scalar.dma_start(bias[:], b.rearrange("(mb p) o -> p (mb o)", p=P))
+        nc.scalar.dma_start(bias[:, :, 0:1], b.rearrange("(mb p) o -> p mb o", p=P))
         nc.sync.dma_start(table_blocks[0][:], table[0:P, :])
         nc.sync.dma_start(weights[0][:, 0, P:M], w_by_row[0:P, 0, P:M])
         nc.sync.dma_start(weights[0][:, 1, :], w_by_row[0:P, 1, :])
@@ -70,7 +70,7 @@ def tile_gather_matmul_kernel(tc, table, w, b, offs, out):
                     results[mb, vb][:, first : first + HALF],
                     banks[mb, vb][:, first : first + HALF],
                     TANH,
-                    bias=bias[:, mb : mb + 1],
+                    bias=bias[:, mb, 0:1],
                 )
                 nc.sync.dma_start(
                     out[mb * P : (mb + 1) * P, vb * PIECE + first : vb * PIECE + first + HALF],

@@ -22,7 +22,6 @@ def tile_gather_matmul_kernel(tc, table, w, b, offs, out):
         tc.psum_pool(name="psum", bufs=1) as psum,
     ):
         offsets = held.tile([P, ENDS * V // 16], U16, align_bytes=ALIGN)
-        nc.sync.dma_start(offsets[:], offs)
 
         table_blocks = [
             held.tile([P, S], BF16, name=f"table{kb}", align_bytes=ALIGN)
@@ -39,6 +38,7 @@ def tile_gather_matmul_kernel(tc, table, w, b, offs, out):
         nc.scalar.dma_start(weights[0][:, 0, 0:P], w_by_row[0:P, 0, 0:P])
         nc.scalar.dma_start(bias[:, :, 0:1], b.rearrange("(mb p) o -> p mb o", p=P))
         nc.sync.dma_start(table_blocks[0][:], table[0:P, :])
+        nc.sync.dma_start(offsets[:], offs)
         nc.sync.dma_start(weights[0][:, 0, P:M], w_by_row[0:P, 0, P:M])
         nc.sync.dma_start(weights[0][:, 1, :], w_by_row[0:P, 1, :])
         nc.sync.dma_start(weights[1][:], w_by_row[P : 2 * P, :, :])

@@ -36,13 +36,13 @@ def tile_gather_matmul_kernel(tc, table, w, b, offs, out):
         w_by_row = w.rearrange("t k m -> k t m")
 
         nc.scalar.dma_start(weights[0][:, 0, 0:P], w_by_row[0:P, 0, 0:P])
-        nc.scalar.dma_start(bias[:, :, 0:1], b.rearrange("(mb p) o -> p mb o", p=P))
         nc.sync.dma_start(table_blocks[0][:], table[0:P, :])
         nc.sync.dma_start(offsets[:], offs)
         nc.sync.dma_start(weights[0][:, 0, P:M], w_by_row[0:P, 0, P:M])
         nc.sync.dma_start(weights[0][:, 1, :], w_by_row[0:P, 1, :])
         nc.sync.dma_start(weights[1][:], w_by_row[P : 2 * P, :, :])
         nc.sync.dma_start(table_blocks[1][:], table[P : 2 * P, :])
+        nc.sync.dma_start(bias[:, :, 0:1], b.rearrange("(mb p) o -> p mb o", p=P))
 
         output_tiles = [(mb, vb) for mb in range(M_BLOCKS) for vb in range(V_BLOCKS)]
         banks = {
@@ -66,13 +66,14 @@ def tile_gather_matmul_kernel(tc, table, w, b, offs, out):
 
         def finish(mb, vb):
             for first in (0, HALF):
+                queue = nc.scalar if (mb, vb) == output_tiles[0] and first == 0 else nc.sync
                 nc.scalar.activation(
                     results[mb, vb][:, first : first + HALF],
                     banks[mb, vb][:, first : first + HALF],
                     TANH,
                     bias=bias[:, mb, 0:1],
                 )
-                nc.sync.dma_start(
+                queue.dma_start(
                     out[mb * P : (mb + 1) * P, vb * PIECE + first : vb * PIECE + first + HALF],
                     results[mb, vb][:, first : first + HALF],
                 )

import concourse.mybir as mybir

BF16, F32, U16 = mybir.dt.bfloat16, mybir.dt.float32, mybir.dt.uint16
TANH = mybir.ActivationFunctionType.Tanh

P = 128
K, S = 256, 4096
ENDS, M = 2, 256
V = 1024
PIECE = 512
K_BLOCKS, M_BLOCKS, V_BLOCKS = K // P, M // P, V // PIECE
ALIGN = 256
HALF = PIECE // 2

FLOPS = 2 * K * M * ENDS * V


def tile_gather_matmul_kernel(tc, table, w, b, offs, out):
    nc = tc.nc
    with (
        tc.tile_pool(name="held", bufs=1) as held,
        tc.psum_pool(name="psum", bufs=1) as psum,
    ):
        offsets = held.tile([P, ENDS * V // 16], U16, align_bytes=ALIGN)

        table_blocks = [
            held.tile([P, S], BF16, name=f"table{kb}", align_bytes=ALIGN)
            for kb in range(K_BLOCKS)
        ]
        weights = [
            held.tile([P, ENDS, M], BF16, name=f"weights{kb}", align_bytes=ALIGN)
            for kb in range(K_BLOCKS)
        ]
        bias = held.tile([P, M_BLOCKS, ALIGN // 4], F32, align_bytes=ALIGN)

        w_by_row = w.rearrange("t k m -> k t m")

        nc.scalar.dma_start(weights[0][:, 0, 0:P], w_by_row[0:P, 0, 0:P])
        nc.sync.dma_start(table_blocks[0][:], table[0:P, :])
        nc.sync.dma_start(offsets[:], offs)
        nc.sync.dma_start(weights[0][:, 0, P:M], w_by_row[0:P, 0, P:M])
        nc.sync.dma_start(weights[0][:, 1, :], w_by_row[0:P, 1, :])
        nc.sync.dma_start(weights[1][:], w_by_row[P : 2 * P, :, :])
        nc.sync.dma_start(table_blocks[1][:], table[P : 2 * P, :])
        nc.sync.dma_start(bias[:, :, 0:1], b.rearrange("(mb p) o -> p mb o", p=P))

        output_tiles = [(mb, vb) for mb in range(M_BLOCKS) for vb in range(V_BLOCKS)]
        banks = {
            (mb, vb): psum.tile([P, PIECE], F32, name=f"bank{mb}{vb}") for mb, vb in output_tiles
        }
        results = {
            (mb, vb): held.tile([P, PIECE], F32, name=f"result{mb}{vb}", align_bytes=ALIGN)
            for mb, vb in output_tiles
        }

        def product(kb, t, mb, vb):
            first_column = (t * V + vb * PIECE) // 16
            piece = offsets[:, first_column : first_column + PIECE // 16]
            nc.tensor.matmul(
                banks[mb, vb][:],
                weights[kb][:, t, mb * P : (mb + 1) * P],
                table_blocks[kb][:].indirect(piece),
                start=(kb == 0 and t == 0),
                stop=(kb == K_BLOCKS - 1 and t == ENDS - 1),
            )

        def finish(mb, vb):
            for first in (0, HALF):
                queue = nc.scalar if (mb, vb) == output_tiles[0] and first == 0 else nc.sync
                nc.scalar.activation(
                    results[mb, vb][:, first : first + HALF],
                    banks[mb, vb][:, first : first + HALF],
                    TANH,
                    bias=bias[:, mb, 0:1],
                )
                queue.dma_start(
                    out[mb * P : (mb + 1) * P, vb * PIECE + first : vb * PIECE + first + HALF],
                    results[mb, vb][:, first : first + HALF],
                )

        for t in range(ENDS):
            for mb, vb in output_tiles:
                product(0, t, mb, vb)
        for mb, vb in output_tiles:
            for t in range(ENDS):
                product(1, t, mb, vb)
            finish(mb, vb)
